import numpy as np
import ml_dtypes


def mxq(x, axis, fmt="e4m3"):
    dtype, down = {"e4m3": (ml_dtypes.float8_e4m3fn, 7), "e5m2": (ml_dtypes.float8_e5m2, 14)}[fmt]
    v = np.moveaxis(np.asarray(x, np.float32).astype(ml_dtypes.bfloat16).astype(np.float64), axis, -1)
    blocks = v.reshape(v.shape[:-1] + (-1, 32))
    amax = np.abs(blocks).max(-1, keepdims=True)
    byte = np.maximum(np.where(amax > 0, np.frexp(amax)[1] - 1 + 127, 0) - down, 1)
    scale = np.exp2(byte - 127.0)
    codes = (blocks / scale).astype(np.float32).astype(dtype).astype(np.float64)
    return np.moveaxis((codes * scale).reshape(v.shape), -1, axis)


WIDE = False


def mx_kscale(k):
    if not WIDE:
        return np.ones(k)
    levels = np.array([10, -10, 5, -5, 0])
    if k % 512:
        return np.exp2(np.random.permutation(np.resize(levels, k // 32))).repeat(32)
    a = np.empty((k // 512, 16))
    for p in range(k // 512):
        a[p, :8] = np.random.permutation(np.resize(levels, 8))
        for g in range(8):
            far = levels[np.abs(levels - a[p, g]) >= 10]
            a[p, g + 8] = far[np.random.randint(len(far))]
    return np.exp2(a.ravel()).repeat(32)


def f64(x):
    return np.asarray(x).astype(np.float64)


def striped(idx):
    return np.tile(np.asarray(idx).reshape(-1, 16).T, (8, 1)).astype(np.uint16)


def unstriped(offs):
    return offs[:16].T.reshape(-1).astype(np.int64)


E2M1 = np.array([0.0, 0.5, 1.0, 1.5, 2.0, 3.0, 4.0, 6.0, -0.0, -0.5, -1.0, -1.5, -2.0, -3.0, -4.0, -6.0])


def pack_weight(w, fmt):
    k, n = w.shape
    w = f64(np.asarray(w, np.float32).astype(ml_dtypes.bfloat16)).reshape(k // 32, 32, n)
    amax = np.abs(w).max(1)
    if fmt == "e4m3":
        byte = np.frexp(amax)[1] - 1 + 127 - 7
    else:
        mant, ex = np.frexp(amax / 6.0)
        byte = np.where(mant > 0.5, ex, ex - 1) + 127
    byte = np.clip(np.where(amax > 0, byte, 1), 1, 254)
    scaled = (w * np.exp2(127.0 - byte)[:, None, :]).reshape(k, n).astype(np.float32)
    by_word = np.ascontiguousarray(scaled.reshape(k // 512, 128, 4, n).transpose(0, 1, 3, 2))
    if fmt == "e4m3":
        words = by_word.astype(ml_dtypes.float8_e4m3fn).view(np.uint8)
    else:
        c = by_word.astype(ml_dtypes.float4_e2m1fn).view(np.uint8) & 0xF
        words = (c[..., 0::2] | (c[..., 1::2] << 4)).reshape(k // 512, 128, 2 * n)
    return np.ascontiguousarray(words), np.ascontiguousarray(byte.astype(np.uint8).reshape(k // 512, 16, n))


def unpack_weight(words, scales, fmt):
    g, _, n = scales.shape
    words = np.ascontiguousarray(words).reshape(g, 128, n, -1)
    if fmt == "e4m3":
        vals = words.view(ml_dtypes.float8_e4m3fn).astype(np.float64)
    else:
        nib = np.empty((g, 128, n, 4), np.uint8)
        nib[..., 0::2] = words & 0xF
        nib[..., 1::2] = words >> 4
        vals = E2M1[nib]
    vals = vals * np.repeat(np.exp2(scales.astype(np.float64) - 127.0), 8, axis=1)[..., None]
    return vals.transpose(0, 1, 3, 2).reshape(g * 512, n)


def bf(x):
    return np.asarray(x, np.float32).astype(ml_dtypes.bfloat16)


def planes(Y):
    r, m = Y.shape
    b = f64(bf(Y)).reshape(r // 32, 32, m)
    amax = np.abs(b).max(1)
    byte = np.clip(np.where(amax > 0, np.frexp(amax)[1] - 1 + 127 - 7, 1), 1, 254)
    codes = (b * np.exp2(127.0 - byte)[:, None, :]).reshape(r, m).astype(np.float32).astype(ml_dtypes.float8_e4m3fn).view(np.uint8)
    words = codes.reshape(r // 512, 128, 4, m).transpose(0, 1, 3, 2)
    return np.ascontiguousarray(words), np.ascontiguousarray(byte.astype(np.uint8).reshape(r // 512, 16, m))


D, T, I, Q, E, X = 512, 2048, 512, 256, 512, 1024


def setup_inputs():
    n = np.random.standard_normal
    idx = np.random.permutation(T)[:I]
    idx2 = np.random.permutation(T)[:I]
    idx3 = np.random.permutation(X)[:I]
    fd = mx_kscale(D)
    fi = mx_kscale(I)
    ti = np.ones(T)
    ti[idx] = fi
    ti3 = np.ones(X)
    ti3[idx3] = fi
    keysp = pack_weight(n((D, T)) / fd[:, None], "e2m1")
    return {
        "query": (n((D, Q)) * 1.0 / np.sqrt(D) * fd[:, None]).astype(np.float32),
        "query2": (n((D, Q)) * 1.0 / np.sqrt(D) * fd[:, None]).astype(np.float32),
        "keys_words": keysp[0],
        "keys_scales": keysp[1],
        "lam": (np.random.uniform(1.0, 3.0, (Q, 1))).astype(np.float32),
        "pull": (np.random.uniform(0.3, 0.9, (Q, 1))).astype(np.float32),
        "os": (np.random.uniform(4.0, 16.0, (1, I)) * fi).astype(np.float32),
        "vals": (n((E, T)) / ti).astype(np.float32),
        "vals2": (n((E, X)) / ti3).astype(np.float32),
        "offs": striped(idx),
        "offs2": striped(idx2),
        "offs3": striped(idx3),
    }


def reference(query, query2, keys_words, keys_scales, lam, pull, os, vals, vals2, offs, offs2, offs3):
    idx = unstriped(offs)
    idx2 = unstriped(offs2)
    idx3 = unstriped(offs3)
    keysu = unpack_weight(keys_words, keys_scales, "e2m1")
    queryq = mxq(f64(query), 0, "e4m3")
    a = queryq.T @ keysu
    query2q = mxq(f64(query2), 0, "e4m3")
    b = query2q.T @ keysu
    la = np.square(a[:, idx]) + np.square(b[:, idx])
    lb = np.square(a[:, idx2]) + np.square(b[:, idx2])
    s = (a[:, idx] * a[:, idx2] + b[:, idx] * b[:, idx2]) / np.sqrt(la * lb + 0.5) * f64(lam)
    p = np.exp(s - np.max(s, axis=1, keepdims=True))
    r = p / np.sum(p, axis=1, keepdims=True)
    r1 = np.pad(r, ((0, 0), (1, 0)))[:, :I]
    w = r - r1 * f64(pull)
    wo1 = np.maximum(w, 0.0) * f64(os)
    wo2 = np.maximum(w * (-1.0), 0.0) * f64(os)
    wt1 = wo1.T
    wt2 = wo2.T
    vt1 = f64(vals)[:, idx].T
    vt2 = f64(vals2)[:, idx3].T
    vt1q = mxq(vt1, 0, "e4m3")
    wt1q = mxq(wt1, 0, "e4m3")
    o = vt1q.T @ wt1q
    vt2q = mxq(vt2, 0, "e4m3")
    wt2q = mxq(wt2, 0, "e4m3")
    o2 = vt2q.T @ wt2q
    y = o - o2
    words, scales = planes(y)
    return y, words, scales

@@ -1,0 +1,262 @@
+from contextlib import ExitStack
+
+import concourse.mybir as mybir
+from concourse.masks import make_identity
+
+D, T, I, Q, E, X = 512, 2048, 512, 256, 512, 1024
+FLOPS = 2 * (2 * Q * T * D + 2 * E * Q * I)
+
+F32 = mybir.dt.float32
+BF16 = mybir.dt.bfloat16
+I32 = mybir.dt.int32
+U32 = mybir.dt.uint32
+U16 = mybir.dt.uint16
+U8 = mybir.dt.uint8
+FP8X4 = mybir.dt.float8_e4m3fn_x4
+FP4X4 = mybir.dt.float4_e2m1fn_x4
+ALU = mybir.AluOpType
+ACT = mybir.ActivationFunctionType
+AX = mybir.AxisListType
+
+P = 128
+PACK = 4
+BANK = 512
+TILES = Q // P
+CHUNKS = T // BANK
+
+
+def tile_attend_planecos_stepwise_bysign_pl_kernel(
+    tc, query, query2, keys_words, keys_scales, lam, pull, slot_factor, vals, vals2, offs, offs2, offs3, out_0, out_1, out_2
+):
+    nc = tc.nc
+    with ExitStack() as ctx:
+        keep = ctx.enter_context(tc.tile_pool(name="keep", bufs=1))
+        psum = ctx.enter_context(tc.psum_pool(name="psum", bufs=1))
+
+        def sb(name, shape, dtype, tag=None):
+            return keep.tile(shape, dtype, name=name, tag=tag or name, align_bytes=64)
+
+        def bank(b, name, shape):
+            return psum.tile(shape, F32, name=name, tag="bank%d" % b)
+
+        key_scales = sb("key_scales", [P, T], U8)
+        nc.gpsimd.memset(key_scales[:].bitcast(U32), 0)
+        q_raw = [sb("q_raw%d" % s, [P, PACK, Q], F32) for s in range(2)]
+        key_words = sb("key_words", [P, 2 * T], U8)
+        lists = [keep.tile([P, I // 16], U16, name="list%d" % s, tag="list%d" % s) for s in range(3)]
+        nc.sync.dma_start(lists[0][:], offs)
+        nc.sync.dma_start(lists[1][:], offs2)
+        nc.sync.dma_start(lists[2][:], offs3)
+        nc.sync.dma_start(out=q_raw[0][:], in_=query.rearrange("(p j) q -> p j q", j=PACK))
+        nc.sync.dma_start(out=key_words[:].bitcast(I32), in_=keys_words[0].bitcast(I32))
+        for g in range(4):
+            nc.sync.dma_start(
+                out=key_scales[32 * g : 32 * g + 4, :].bitcast(I32), in_=keys_scales[0][4 * g : 4 * g + 4, :].bitcast(I32)
+            )
+        nc.sync.dma_start(out=q_raw[1][:], in_=query2.rearrange("(p j) q -> p j q", j=PACK))
+        pools = []
+        for s, width in enumerate((T, X)):
+            pools.append([sb("pool%d_%d" % (s, j), [P, width], F32) for j in range(PACK)])
+        lam_col = sb("lam_col", [P, TILES], F32, tag="got0")
+        pull_col = sb("pull_col", [P, TILES], F32)
+        factor = sb("factor", [P, PACK], F32)
+        for j in range(PACK):
+            nc.sync.dma_start(out=pools[1][j][:], in_=vals2.rearrange("(p j) t -> p j t", j=PACK)[:, j, :])
+        with nc.allow_non_contiguous_dma(reason="one number a query row"):
+            nc.sync.dma_start(out=lam_col[:], in_=lam.rearrange("(t p) o -> p (t o)", p=P))
+            nc.sync.dma_start(out=pull_col[:], in_=pull.rearrange("(t p) o -> p (t o)", p=P))
+        nc.sync.dma_start(out=factor[:], in_=slot_factor.rearrange("o (p t) -> p (o t)", t=PACK))
+        for j in range(PACK):
+            nc.sync.dma_start(out=pools[0][j][:], in_=vals.rearrange("(p j) t -> p j t", j=PACK)[:, j, :])
+
+        warm = sb("warm", [P, 2], F32)
+        nc.vector.memset(warm[:, 0:1], 1.0)
+        nc.scalar.activation(out=warm[:, 1:2], in_=warm[:, 0:1], func=ACT.Abs_reciprocal_sqrt)
+        ident = sb("ident", [P, P], F32)
+        make_identity(nc, ident[:])
+        shares = [sb("shares%d" % n, [P, PACK, P + 1], F32) for n in range(TILES)]
+        for n in range(TILES):
+            nc.gpsimd.memset(shares[n][:, :, 0:1], 0.0)
+        neg_pull = sb("neg_pull", [P, TILES], F32)
+        nc.gpsimd.tensor_scalar(out=neg_pull[:], in0=pull_col[:], scalar1=-1.0, scalar2=0.0, op0=ALU.mult, op1=ALU.add)
+
+        q_codes, q_scales = {}, {}
+        for s, n in ((0, 0), (1, 0), (0, 1), (1, 1)):
+            grouped = sb("q_grouped%d%d" % (s, n), [P, P, PACK], BF16)
+            nc.vector.tensor_copy(out=grouped[:], in_=q_raw[s][:, :, n * P : (n + 1) * P].rearrange("p j q -> p q j"))
+            q_codes[s, n] = sb("q_codes%d%d" % (s, n), [P, P], U32)
+            q_scales[s, n] = sb("q_scales%d%d" % (s, n), [P, P], U8)
+            nc.vector.quantize_mx(
+                out=q_codes[s, n][:].bitcast(FP8X4), scales=q_scales[s, n][:], in_=grouped[:].rearrange("p q j -> p (q j)")
+            )
+
+        points = {}
+        picked = [sb("picked%d" % n, [P, 4, I], F32) for n in range(TILES)]
+        squares = [sb("squares%d" % n, [P, 4, I], F32) for n in range(TILES)]
+        for n in range(TILES):
+            for s in range(2):
+                points[s, n] = sb("points%d%d" % (s, n), [P, T], F32)
+                for c in range(CHUNKS):
+                    acc = bank(c, "acc", [P, BANK])
+                    nc.tensor.matmul_mx(
+                        out=acc[:],
+                        lhsT=q_codes[s, n][:].bitcast(FP8X4),
+                        lhsT_scale=q_scales[s, n][:],
+                        rhs=key_words[:, 2 * c * BANK : 2 * (c + 1) * BANK].bitcast(FP4X4),
+                        rhs_scale=key_scales[:, c * BANK : (c + 1) * BANK],
+                        start=True,
+                        stop=True,
+                    )
+                    dst = points[s, n][:, c * BANK : (c + 1) * BANK]
+                    if (n, s) == (0, 0) and c % 2 == 1:
+                        nc.vector.tensor_copy(out=dst, in_=acc[:])
+                    else:
+                        nc.scalar.copy(out=dst, in_=acc[:])
+                for k in range(2):
+                    nc.vector.tensor_copy(out=picked[n][:, 2 * s + k, :], in_=points[s, n][:].indirect(lists[k][:]))
+
+        def turn_sum(dst, first, second):
+            for c in range(PACK):
+                cols = slice(c * P, (c + 1) * P)
+                nc.tensor.matmul(dst[:, c, :], first[:, cols], ident[:], start=True, stop=False, is_transpose=True)
+                nc.tensor.matmul(dst[:, c, :], second[:, cols], ident[:], start=False, stop=True, is_transpose=True)
+
+        base = (4, 0)
+        dots, inv = [], []
+        for n in range(TILES):
+            for s in range(2):
+                nc.scalar.activation(out=squares[n][:, 2 * s : 2 * s + 2, :], in_=picked[n][:, 2 * s : 2 * s + 2, :], func=ACT.Square)
+            products = sb("products%d" % n, [P, 2, I], F32, tag=("points11", None)[n])
+            nc.vector.scalar_tensor_tensor(
+                out=products[:], in0=picked[n][:, 0::2, :], scalar=lam_col[:, n : n + 1], in1=picked[n][:, 1::2, :],
+                op0=ALU.mult, op1=ALU.mult,
+            )
+            la = bank(base[n], "la", [P, PACK, P])
+            lb = bank(base[n] + 1, "lb", [P, PACK, P])
+            dot = bank(base[n] + 2, "dot", [P, PACK, P])
+            turn_sum(la, squares[n][:, 0, :], squares[n][:, 2, :])
+            turn_sum(lb, squares[n][:, 1, :], squares[n][:, 3, :])
+            turn_sum(dot, products[:, 0, :], products[:, 1, :])
+            la_sb = sb("la_sb%d" % n, [P, PACK, P], F32, tag=("got1", None)[n])
+            nc.scalar.copy(out=la_sb[:], in_=la[:])
+            lengths = sb("lengths%d" % n, [P, PACK, P], F32, tag=(None, "got5")[n])
+            nc.vector.tensor_tensor(out=lengths[:], in0=lb[:], in1=la_sb[:], op=ALU.mult)
+            root = sb("root%d" % n, [P, PACK, P], F32, tag=("got2", "got3")[n])
+            nc.scalar.activation(out=root[:], in_=lengths[:], func=ACT.Abs_reciprocal_sqrt, bias=0.5)
+            dots.append(dot)
+            inv.append(root)
+
+        scores, neg_max = [], []
+        for n in range(TILES):
+            turned = sb("turned%d" % n, [P, PACK, P], F32, tag=(None, "got4")[n])
+            nc.vector.tensor_tensor(out=turned[:], in0=dots[n][:], in1=inv[n][:], op=ALU.mult)
+            score = bank(base[n], "score", [P, PACK, P])
+            for c in range(PACK):
+                nc.tensor.transpose(score[:, c, :], turned[:, c, :], ident[:])
+            top = sb("top%d" % n, [P, 1], F32)
+            nc.vector.tensor_reduce(out=top[:], in_=score[:], axis=AX.XY, op=ALU.max, negate=True)
+            scores.append(score)
+            neg_max.append(top)
+
+        v_codes, v_scales = {}, {}
+
+        def values(s, h, tags):
+            turned_v = bank((7, 3)[h], "turned_v", [P, 2, 2, P])
+            both = len(tags) == 1
+            got = sb("got%d%d" % (s, h), [P, 2 * I if both else I], BF16, tag=tags[0])
+            for jj in range(2):
+                j = 2 * h + jj
+                if both:
+                    dst = got[:, jj * I : (jj + 1) * I]
+                else:
+                    if jj == 1:
+                        got = sb("got%d%dx" % (s, h), [P, I], BF16, tag=tags[1])
+                    dst = got[:]
+                nc.vector.tensor_copy(out=dst, in_=pools[s][j][:].indirect(lists[2 * s][:]))
+                words = dst.bitcast(F32)
+                for u in range(2):
+                    nc.tensor.transpose(turned_v[:, jj, u, :], words[:, u::2], ident[:])
+            v_grouped = sb("v_grouped%d%d" % (s, h), [P, 2 * P * PACK], BF16)
+            nc.scalar.copy(
+                out=v_grouped[:].bitcast(F32).rearrange("p (j m u) -> p j m u", j=2, u=2),
+                in_=turned_v[:].rearrange("p j u m -> p j m u"),
+            )
+            v_codes[s, h] = sb("v_codes%d%d" % (s, h), [P, 2 * P], U32)
+            v_scales[s, h] = sb("v_scales%d%d" % (s, h), [P, 2 * P], U8)
+            nc.vector.quantize_mx(out=v_codes[s, h][:].bitcast(FP8X4), scales=v_scales[s, h][:], in_=v_grouped[:])
+
+        values(1, 0, ("got0", "got1"))
+        values(1, 1, ("got2", "got3"))
+        norms = []
+        for n in range(TILES):
+            total = sb("total%d" % n, [P, 1], F32, tag=("got5", "got6")[n])
+            nc.scalar.activation(
+                out=shares[n][:, :, 1 : P + 1], in_=scores[n][:].rearrange("q c p -> q (c p)").rearrange("q (p t) -> q t p", t=PACK), func=ACT.Exp,
+                bias=neg_max[n][:], accum_out=total[:],
+            )
+            norm = sb("norm%d" % n, [P, 1], F32)
+            nc.vector.reciprocal(out=norm[:], in_=total[:])
+            norms.append(norm)
+        weights = []
+        for n in range(TILES):
+            share = sb("share%d" % n, [P, PACK, P + 1], F32)
+            pulled = sb("pulled%d" % n, [P, PACK, P + 1], F32)
+            nc.scalar.activation(out=share[:], in_=shares[n][:], func=ACT.Copy, scale=norms[n][:])
+            nc.scalar.activation(out=pulled[:], in_=share[:], func=ACT.Copy, scale=neg_pull[:, n : n + 1])
+            turned_w = bank(base[n] + 1, "weights", [P, PACK, P])
+            for t in range(PACK):
+                before = pulled[:, t - 1, 1 : P + 1] if t > 0 else pulled[:, PACK - 1, 0:P]
+                nc.tensor.matmul(turned_w[:, t, :], share[:, t, 1 : P + 1], ident[:], start=True, stop=False, is_transpose=True)
+                nc.tensor.matmul(turned_w[:, t, :], before, ident[:], start=False, stop=True, is_transpose=True)
+            weights.append(turned_w)
+        values(0, 0, ("got4", "got5"))
+        values(0, 1, ("got6",))
+
+        y_codes = sb("y_codes", [P, Q], U32)
+        y_scales = sb("y_scales", [P, Q], U8)
+        for n in range(TILES):
+            w_grouped = sb("w_grouped%d" % n, [P, 2, P, PACK], BF16)
+            for s, op in enumerate((ALU.max, ALU.min)):
+                nc.vector.scalar_tensor_tensor(
+                    out=w_grouped[:, s, :, :], in0=weights[n][:].rearrange("p t q -> p q t"), scalar=0.0,
+                    in1=factor[:].unsqueeze(1).to_broadcast([P, P, PACK]), op0=op, op1=ALU.mult,
+                )
+            w_codes = sb("w_codes%d" % n, [P, 2 * P], U32)
+            w_scales = sb("w_scales%d" % n, [P, 2 * P], U8)
+            nc.vector.quantize_mx(
+                out=w_codes[:].bitcast(FP8X4), scales=w_scales[:], in_=w_grouped[:].rearrange("p s q t -> p (s q t)")
+            )
+            result = bank(base[n] + 2, "result", [P, PACK, P])
+            for j in range(PACK):
+                h, jj = divmod(j, 2)
+                for s in range(2):
+                    nc.tensor.matmul_mx(
+                        out=result[:, j, :],
+                        lhsT=v_codes[s, h][:, jj * P : (jj + 1) * P].bitcast(FP8X4),
+                        lhsT_scale=v_scales[s, h][:, jj * P : (jj + 1) * P],
+                        rhs=w_codes[:, s * P : (s + 1) * P].bitcast(FP8X4),
+                        rhs_scale=w_scales[:, s * P : (s + 1) * P],
+                        start=(s == 0),
+                        stop=(s == 1),
+                    )
+            cols = slice(n * P, (n + 1) * P)
+            y_grouped = sb("y_grouped%d" % n, [P, P, PACK], BF16)
+            if n == 0:
+                nc.scalar.copy(out=y_grouped[:], in_=result[:].rearrange("p j q -> p q j"))
+            else:
+                nc.vector.tensor_copy(out=y_grouped[:], in_=result[:].rearrange("p j q -> p q j"))
+            y_out = sb("y_out%d" % n, [P, PACK, P], F32)
+            nc.scalar.copy(out=y_out[:], in_=result[:])
+            nc.sync.dma_start(out=out_0.rearrange("(p j) q -> p j q", j=PACK)[:, :, cols], in_=y_out[:])
+            nc.vector.quantize_mx(
+                out=y_codes[:, cols].bitcast(FP8X4), scales=y_scales[:, cols], in_=y_grouped[:].rearrange("p q j -> p (q j)")
+            )
+            nc.sync.dma_start(
+                out=out_1[0].rearrange("p q r -> p (q r)")[:, 4 * n * P : 4 * (n + 1) * P].bitcast(I32),
+                in_=y_codes[:, cols].bitcast(I32),
+            )
+        for g in range(4):
+            queue = (nc.sync, nc.scalar)[g % 2]
+            queue.dma_start(
+                out=out_2[0][4 * g : 4 * g + 4, :].bitcast(I32), in_=y_scales[32 * g : 32 * g + 4, :].bitcast(I32)
+            )

@@ -41,23 +41,30 @@ def tile_attend_planecos_stepwise_bysign_pl_kernel(
 
         key_scales = sb("key_scales", [P, T], U8)
         nc.gpsimd.memset(key_scales[:].bitcast(U32), 0)
-        q_raw = [sb("q_raw%d" % s, [P, PACK, Q], F32) for s in range(2)]
+        q_raw = {(s, n): sb("q_raw%d%d" % (s, n), [P, PACK, P], F32) for s in range(2) for n in range(TILES)}
+
+        def load_queries(s, n):
+            src = (query, query2)[s].rearrange("(p j) q -> p j q", j=PACK)
+            nc.sync.dma_start(out=q_raw[s, n][:], in_=src[:, :, n * P : (n + 1) * P])
+
         key_words = sb("key_words", [P, 2 * T], U8)
         lists = [keep.tile([P, I // 16], U16, name="list%d" % s, tag="list%d" % s) for s in range(3)]
         nc.sync.dma_start(lists[0][:], offs)
         nc.sync.dma_start(lists[1][:], offs2)
         nc.sync.dma_start(lists[2][:], offs3)
-        nc.sync.dma_start(out=q_raw[0][:], in_=query.rearrange("(p j) q -> p j q", j=PACK))
+        load_queries(0, 0)
         nc.sync.dma_start(out=key_words[:].bitcast(I32), in_=keys_words[0].bitcast(I32))
         for g in range(4):
             nc.sync.dma_start(
                 out=key_scales[32 * g : 32 * g + 4, :].bitcast(I32), in_=keys_scales[0][4 * g : 4 * g + 4, :].bitcast(I32)
             )
-        nc.sync.dma_start(out=q_raw[1][:], in_=query2.rearrange("(p j) q -> p j q", j=PACK))
+        load_queries(1, 0)
+        load_queries(0, 1)
+        load_queries(1, 1)
         pools = []
         for s, width in enumerate((T, X)):
             pools.append([sb("pool%d_%d" % (s, j), [P, width], F32) for j in range(PACK)])
-        lam_col = sb("lam_col", [P, TILES], F32, tag="got0")
+        lam_col = sb("lam_col", [P, TILES], F32)
         pull_col = sb("pull_col", [P, TILES], F32)
         factor = sb("factor", [P, PACK], F32)
         for j in range(PACK):
@@ -80,10 +87,27 @@ def tile_attend_planecos_stepwise_bysign_pl_kernel(
         neg_pull = sb("neg_pull", [P, TILES], F32)
         nc.gpsimd.tensor_scalar(out=neg_pull[:], in0=pull_col[:], scalar1=-1.0, scalar2=0.0, op0=ALU.mult, op1=ALU.add)
 
+        neg_lam = sb("neg_lam", [P, TILES], F32, tag="got6")
+        nc.gpsimd.tensor_scalar(out=neg_lam[:], in0=lam_col[:], scalar1=-1.0, scalar2=0.0, op0=ALU.mult, op1=ALU.add)
+        minus_one = sb("minus_one", [P, 1], F32)
+        nc.gpsimd.memset(minus_one[:], -1.0)
+        got = {}
+        rounded = {0: sb("rounded0", [P, X], BF16)}
+        for c in range(2):
+            nc.gpsimd.tensor_copy(out=rounded[0][:, c * BANK : (c + 1) * BANK], in_=pools[1][0][:, c * BANK : (c + 1) * BANK])
+
+        def gather_on_scalar(j, tag):
+            got[1, j] = sb("got1%d" % j, [P, I], BF16, tag=tag)
+            nc.scalar.activation(out=got[1, j][:], in_=rounded[j][:].indirect(lists[2][:]), func=ACT.Copy)
+
+        def gather_on_vector(s, j, tag):
+            got[s, j] = sb("got%d%d" % (s, j), [P, I], BF16, tag=tag)
+            nc.vector.tensor_copy(out=got[s, j][:], in_=pools[s][j][:].indirect(lists[2 * s][:]))
+
         q_codes, q_scales = {}, {}
         for s, n in ((0, 0), (1, 0), (0, 1), (1, 1)):
             grouped = sb("q_grouped%d%d" % (s, n), [P, P, PACK], BF16)
-            nc.vector.tensor_copy(out=grouped[:], in_=q_raw[s][:, :, n * P : (n + 1) * P].rearrange("p j q -> p q j"))
+            nc.vector.tensor_copy(out=grouped[:], in_=q_raw[s, n][:].rearrange("p j q -> p q j"))
             q_codes[s, n] = sb("q_codes%d%d" % (s, n), [P, P], U32)
             q_scales[s, n] = sb("q_scales%d%d" % (s, n), [P, P], U8)
             nc.vector.quantize_mx(
@@ -121,59 +145,76 @@ def tile_attend_planecos_stepwise_bysign_pl_kernel(
                 nc.tensor.matmul(dst[:, c, :], first[:, cols], ident[:], start=True, stop=False, is_transpose=True)
                 nc.tensor.matmul(dst[:, c, :], second[:, cols], ident[:], start=False, stop=True, is_transpose=True)
 
-        base = (4, 0)
-        dots, inv = [], []
-        for n in range(TILES):
-            for s in range(2):
-                nc.scalar.activation(out=squares[n][:, 2 * s : 2 * s + 2, :], in_=picked[n][:, 2 * s : 2 * s + 2, :], func=ACT.Square)
-            products = sb("products%d" % n, [P, 2, I], F32, tag=("points11", None)[n])
-            nc.vector.scalar_tensor_tensor(
-                out=products[:], in0=picked[n][:, 0::2, :], scalar=lam_col[:, n : n + 1], in1=picked[n][:, 1::2, :],
-                op0=ALU.mult, op1=ALU.mult,
-            )
-            la = bank(base[n], "la", [P, PACK, P])
-            lb = bank(base[n] + 1, "lb", [P, PACK, P])
-            dot = bank(base[n] + 2, "dot", [P, PACK, P])
-            turn_sum(la, squares[n][:, 0, :], squares[n][:, 2, :])
-            turn_sum(lb, squares[n][:, 1, :], squares[n][:, 3, :])
-            turn_sum(dot, products[:, 0, :], products[:, 1, :])
-            la_sb = sb("la_sb%d" % n, [P, PACK, P], F32, tag=("got1", None)[n])
-            nc.scalar.copy(out=la_sb[:], in_=la[:])
-            lengths = sb("lengths%d" % n, [P, PACK, P], F32, tag=(None, "got5")[n])
-            nc.vector.tensor_tensor(out=lengths[:], in0=lb[:], in1=la_sb[:], op=ALU.mult)
-            root = sb("root%d" % n, [P, PACK, P], F32, tag=("got2", "got3")[n])
-            nc.scalar.activation(out=root[:], in_=lengths[:], func=ACT.Abs_reciprocal_sqrt, bias=0.5)
-            dots.append(dot)
-            inv.append(root)
+        base = (4, 6)
+        dots, inv, las, lbs, lengths = {}, {}, {}, {}, {}
 
+        def square(n, first, count):
+            part = picked[n][:, first : first + count, :]
+            if n == 0:
+                nc.gpsimd.tensor_tensor(out=squares[n][:, first : first + count, :], in0=part, in1=part, op=ALU.mult)
+            else:
+                nc.scalar.activation(out=squares[n][:, first : first + count, :], in_=part, func=ACT.Square)
+
+        def sum_first(n):
+            la = bank(base[n], "la", [P, PACK, P])
+            turn_sum(la, squares[n][:, 0, :], squares[n][:, 2, :])
+            las[n] = sb("la_sb%d" % n, [P, PACK, P], F32, tag=("got2", "got8")[n])
+            nc.scalar.copy(out=las[n][:], in_=la[:])
+
+        def sum_second(n):
+            lbs[n] = bank(base[n] + 1, "lb", [P, PACK, P])
+            turn_sum(lbs[n], squares[n][:, 1, :], squares[n][:, 3, :])
+
+        def dot_product(n):
+            products = sb("products%d" % n, [P, 2, I], F32)
+            for s in range(2):
+                nc.gpsimd.tensor_tensor(out=products[:, s, :], in0=picked[n][:, 2 * s, :], in1=picked[n][:, 2 * s + 1, :], op=ALU.mult)
+            dots[n] = bank(base[n], "dot", [P, PACK, P])
+            turn_sum(dots[n], products[:, 0, :], products[:, 1, :])
+
+        def inverse_root(n):
+            lengths[n] = sb("lengths%d" % n, [P, PACK, P], F32, tag=(None, "got7")[n])
+            nc.vector.tensor_tensor(out=lengths[n][:], in0=lbs[n][:], in1=las[n][:], op=ALU.mult)
+            inv[n] = sb("root%d" % n, [P, PACK, P], F32, tag=("got3", "got4")[n])
+            nc.scalar.activation(out=inv[n][:], in_=lengths[n][:], func=ACT.Abs_reciprocal_sqrt, bias=0.5)
+
+        gather_on_vector(1, 2, "points10")
+        square(0, 0, 2)
+        square(0, 2, 2)
+        sum_first(0)
+        sum_second(0)
+        square(1, 0, 2)
+        square(1, 2, 1)
+        sum_first(1)
+        square(1, 3, 1)
+        sum_second(1)
+        dot_product(0)
+        inverse_root(0)
+        inverse_root(1)
+        dot_product(1)
+        gather_on_scalar(0, "squares1")
         scores, neg_max = [], []
         for n in range(TILES):
-            turned = sb("turned%d" % n, [P, PACK, P], F32, tag=(None, "got4")[n])
+            turned = sb("turned%d" % n, [P, PACK, P], F32)
             nc.vector.tensor_tensor(out=turned[:], in0=dots[n][:], in1=inv[n][:], op=ALU.mult)
-            score = bank(base[n], "score", [P, PACK, P])
+            score = bank(n, "score", [P, PACK, P])
             for c in range(PACK):
                 nc.tensor.transpose(score[:, c, :], turned[:, c, :], ident[:])
             top = sb("top%d" % n, [P, 1], F32)
-            nc.vector.tensor_reduce(out=top[:], in_=score[:], axis=AX.XY, op=ALU.max, negate=True)
-            scores.append(score)
+            neg_score = sb("neg_score%d" % n, [P, PACK, P], F32)
+            nc.vector.tensor_scalar(
+                out=neg_score[:], in0=score[:].rearrange("q c p -> q (c p)").rearrange("q (p t) -> q t p", t=PACK),
+                scalar1=neg_lam[:, n : n + 1], scalar2=None, op0=ALU.mult, op1=ALU.min, accum_out=top[:],
+            )
+            scores.append(neg_score)
             neg_max.append(top)
 
         v_codes, v_scales = {}, {}
 
-        def values(s, h, tags):
-            turned_v = bank((7, 3)[h], "turned_v", [P, 2, 2, P])
-            both = len(tags) == 1
-            got = sb("got%d%d" % (s, h), [P, 2 * I if both else I], BF16, tag=tags[0])
+        def values(s, h):
+            turned_v = bank({(1, 0): 4, (1, 1): 7, (0, 0): 1, (0, 1): 3}[s, h], "turned_v", [P, 2, 2, P])
             for jj in range(2):
-                j = 2 * h + jj
-                if both:
-                    dst = got[:, jj * I : (jj + 1) * I]
-                else:
-                    if jj == 1:
-                        got = sb("got%d%dx" % (s, h), [P, I], BF16, tag=tags[1])
-                    dst = got[:]
-                nc.vector.tensor_copy(out=dst, in_=pools[s][j][:].indirect(lists[2 * s][:]))
-                words = dst.bitcast(F32)
+                words = got[s, 2 * h + jj][:].bitcast(F32)
                 for u in range(2):
                     nc.tensor.transpose(turned_v[:, jj, u, :], words[:, u::2], ident[:])
             v_grouped = sb("v_grouped%d%d" % (s, h), [P, 2 * P * PACK], BF16)
@@ -185,32 +226,40 @@ def tile_attend_planecos_stepwise_bysign_pl_kernel(
             v_scales[s, h] = sb("v_scales%d%d" % (s, h), [P, 2 * P], U8)
             nc.vector.quantize_mx(out=v_codes[s, h][:].bitcast(FP8X4), scales=v_scales[s, h][:], in_=v_grouped[:])
 
-        values(1, 0, ("got0", "got1"))
-        values(1, 1, ("got2", "got3"))
+        gather_on_vector(1, 3, "got2")
+        gather_on_vector(1, 1, "got3")
+        gather_on_vector(0, 0, "got8")
+        gather_on_vector(0, 1, "got4")
+        gather_on_vector(0, 2, "got6")
         norms = []
         for n in range(TILES):
-            total = sb("total%d" % n, [P, 1], F32, tag=("got5", "got6")[n])
+            total = sb("total%d" % n, [P, 1], F32, tag=("got7", None)[n])
             nc.scalar.activation(
-                out=shares[n][:, :, 1 : P + 1], in_=scores[n][:].rearrange("q c p -> q (c p)").rearrange("q (p t) -> q t p", t=PACK), func=ACT.Exp,
+                out=shares[n][:, :, 1 : P + 1], in_=scores[n][:], func=ACT.Exp, scale=-1.0,
                 bias=neg_max[n][:], accum_out=total[:],
             )
             norm = sb("norm%d" % n, [P, 1], F32)
-            nc.vector.reciprocal(out=norm[:], in_=total[:])
+            nc.gpsimd.tensor_tensor(out=norm[:], in0=total[:], in1=minus_one[:], op=ALU.pow)
             norms.append(norm)
         weights = []
         for n in range(TILES):
             share = sb("share%d" % n, [P, PACK, P + 1], F32)
             pulled = sb("pulled%d" % n, [P, PACK, P + 1], F32)
             nc.scalar.activation(out=share[:], in_=shares[n][:], func=ACT.Copy, scale=norms[n][:])
-            nc.scalar.activation(out=pulled[:], in_=share[:], func=ACT.Copy, scale=neg_pull[:, n : n + 1])
-            turned_w = bank(base[n] + 1, "weights", [P, PACK, P])
+            nc.gpsimd.tensor_scalar(
+                out=pulled[:], in0=shares[n][:], scalar1=norms[n][:], scalar2=neg_pull[:, n : n + 1], op0=ALU.mult, op1=ALU.mult
+            )
+            turned_w = bank((2, 6)[n], "weights", [P, PACK, P])
             for t in range(PACK):
                 before = pulled[:, t - 1, 1 : P + 1] if t > 0 else pulled[:, PACK - 1, 0:P]
                 nc.tensor.matmul(turned_w[:, t, :], share[:, t, 1 : P + 1], ident[:], start=True, stop=False, is_transpose=True)
                 nc.tensor.matmul(turned_w[:, t, :], before, ident[:], start=False, stop=True, is_transpose=True)
             weights.append(turned_w)
-        values(0, 0, ("got4", "got5"))
-        values(0, 1, ("got6",))
+        gather_on_vector(0, 3, "shares0")
+        values(1, 1)
+        values(1, 0)
+        values(0, 0)
+        values(0, 1)
 
         y_codes = sb("y_codes", [P, Q], U32)
         y_scales = sb("y_scales", [P, Q], U8)
@@ -226,7 +275,7 @@ def tile_attend_planecos_stepwise_bysign_pl_kernel(
             nc.vector.quantize_mx(
                 out=w_codes[:].bitcast(FP8X4), scales=w_scales[:], in_=w_grouped[:].rearrange("p s q t -> p (s q t)")
             )
-            result = bank(base[n] + 2, "result", [P, PACK, P])
+            result = bank((0, 5)[n], "result", [P, PACK, P])
             for j in range(PACK):
                 h, jj = divmod(j, 2)
                 for s in range(2):

@@ -87,14 +87,9 @@ def tile_attend_planecos_stepwise_bysign_pl_kernel(
         neg_pull = sb("neg_pull", [P, TILES], F32)
         nc.gpsimd.tensor_scalar(out=neg_pull[:], in0=pull_col[:], scalar1=-1.0, scalar2=0.0, op0=ALU.mult, op1=ALU.add)
 
-        neg_lam = sb("neg_lam", [P, TILES], F32, tag="got6")
+        neg_lam = sb("neg_lam", [P, TILES], F32)
         nc.gpsimd.tensor_scalar(out=neg_lam[:], in0=lam_col[:], scalar1=-1.0, scalar2=0.0, op0=ALU.mult, op1=ALU.add)
-        minus_one = sb("minus_one", [P, 1], F32)
-        nc.gpsimd.memset(minus_one[:], -1.0)
         got = {}
-        rounded = {0: sb("rounded0", [P, X], BF16)}
-        for c in range(2):
-            nc.gpsimd.tensor_copy(out=rounded[0][:, c * BANK : (c + 1) * BANK], in_=pools[1][0][:, c * BANK : (c + 1) * BANK])
 
         def gather_on_scalar(j, tag):
             got[1, j] = sb("got1%d" % j, [P, I], BF16, tag=tag)
@@ -113,6 +108,10 @@ def tile_attend_planecos_stepwise_bysign_pl_kernel(
             nc.vector.quantize_mx(
                 out=q_codes[s, n][:].bitcast(FP8X4), scales=q_scales[s, n][:], in_=grouped[:].rearrange("p q j -> p (q j)")
             )
+
+        rounded = {0: sb("rounded0", [P, X], BF16, tag="q_grouped11")}
+        for c in range(2):
+            nc.gpsimd.tensor_copy(out=rounded[0][:, c * BANK : (c + 1) * BANK], in_=pools[1][0][:, c * BANK : (c + 1) * BANK])
 
         points = {}
         picked = [sb("picked%d" % n, [P, 4, I], F32) for n in range(TILES)]
@@ -169,7 +168,7 @@ def tile_attend_planecos_stepwise_bysign_pl_kernel(
             products = sb("products%d" % n, [P, 2, I], F32)
             for s in range(2):
                 nc.gpsimd.tensor_tensor(out=products[:, s, :], in0=picked[n][:, 2 * s, :], in1=picked[n][:, 2 * s + 1, :], op=ALU.mult)
-            dots[n] = bank(base[n], "dot", [P, PACK, P])
+            dots[n] = bank(4, "dot", [P, PACK, P])
             turn_sum(dots[n], products[:, 0, :], products[:, 1, :])
 
         def inverse_root(n):
@@ -178,23 +177,9 @@ def tile_attend_planecos_stepwise_bysign_pl_kernel(
             inv[n] = sb("root%d" % n, [P, PACK, P], F32, tag=("got3", "got4")[n])
             nc.scalar.activation(out=inv[n][:], in_=lengths[n][:], func=ACT.Abs_reciprocal_sqrt, bias=0.5)
 
-        gather_on_vector(1, 2, "points10")
-        square(0, 0, 2)
-        square(0, 2, 2)
-        sum_first(0)
-        sum_second(0)
-        square(1, 0, 2)
-        square(1, 2, 1)
-        sum_first(1)
-        square(1, 3, 1)
-        sum_second(1)
-        dot_product(0)
-        inverse_root(0)
-        inverse_root(1)
-        dot_product(1)
-        gather_on_scalar(0, "squares1")
         scores, neg_max = [], []
-        for n in range(TILES):
+
+        def row_scores(n):
             turned = sb("turned%d" % n, [P, PACK, P], F32)
             nc.vector.tensor_tensor(out=turned[:], in0=dots[n][:], in1=inv[n][:], op=ALU.mult)
             score = bank(n, "score", [P, PACK, P])
@@ -209,15 +194,32 @@ def tile_attend_planecos_stepwise_bysign_pl_kernel(
             scores.append(neg_score)
             neg_max.append(top)
 
+        gather_on_vector(1, 2, "points10")
+        square(0, 0, 2)
+        square(0, 2, 2)
+        sum_first(0)
+        sum_second(0)
+        square(1, 0, 2)
+        square(1, 2, 1)
+        sum_first(1)
+        square(1, 3, 1)
+        sum_second(1)
+        dot_product(0)
+        inverse_root(0)
+        inverse_root(1)
+        row_scores(0)
+        dot_product(1)
+        row_scores(1)
+        gather_on_scalar(0, "squares1")
         v_codes, v_scales = {}, {}
 
         def values(s, h):
-            turned_v = bank({(1, 0): 4, (1, 1): 7, (0, 0): 1, (0, 1): 3}[s, h], "turned_v", [P, 2, 2, P])
+            turned_v = bank({(1, 0): 6, (1, 1): 7, (0, 0): 1, (0, 1): 1}[s, h], "turned_v", [P, 2, 2, P])
             for jj in range(2):
                 words = got[s, 2 * h + jj][:].bitcast(F32)
                 for u in range(2):
                     nc.tensor.transpose(turned_v[:, jj, u, :], words[:, u::2], ident[:])
-            v_grouped = sb("v_grouped%d%d" % (s, h), [P, 2 * P * PACK], BF16)
+            v_grouped = sb("v_grouped%d%d" % (s, h), [P, 2 * P * PACK], BF16, tag={(0, 0): "neg_score1", (0, 1): "share0"}.get((s, h)))
             nc.scalar.copy(
                 out=v_grouped[:].bitcast(F32).rearrange("p (j m u) -> p j m u", j=2, u=2),
                 in_=turned_v[:].rearrange("p j u m -> p j m u"),
@@ -230,32 +232,30 @@ def tile_attend_planecos_stepwise_bysign_pl_kernel(
         gather_on_vector(1, 1, "got3")
         gather_on_vector(0, 0, "got8")
         gather_on_vector(0, 1, "got4")
-        gather_on_vector(0, 2, "got6")
-        norms = []
+        norms, weights = [], []
         for n in range(TILES):
-            total = sb("total%d" % n, [P, 1], F32, tag=("got7", None)[n])
+            total = sb("total%d" % n, [P, 1], F32, tag=("got7", "got6")[n])
             nc.scalar.activation(
                 out=shares[n][:, :, 1 : P + 1], in_=scores[n][:], func=ACT.Exp, scale=-1.0,
                 bias=neg_max[n][:], accum_out=total[:],
             )
             norm = sb("norm%d" % n, [P, 1], F32)
-            nc.gpsimd.tensor_tensor(out=norm[:], in0=total[:], in1=minus_one[:], op=ALU.pow)
+            nc.vector.reciprocal(out=norm[:], in_=total[:])
             norms.append(norm)
-        weights = []
-        for n in range(TILES):
             share = sb("share%d" % n, [P, PACK, P + 1], F32)
             pulled = sb("pulled%d" % n, [P, PACK, P + 1], F32)
             nc.scalar.activation(out=share[:], in_=shares[n][:], func=ACT.Copy, scale=norms[n][:])
             nc.gpsimd.tensor_scalar(
                 out=pulled[:], in0=shares[n][:], scalar1=norms[n][:], scalar2=neg_pull[:, n : n + 1], op0=ALU.mult, op1=ALU.mult
             )
-            turned_w = bank((2, 6)[n], "weights", [P, PACK, P])
+            turned_w = bank((2, 4)[n], "weights", [P, PACK, P])
             for t in range(PACK):
                 before = pulled[:, t - 1, 1 : P + 1] if t > 0 else pulled[:, PACK - 1, 0:P]
                 nc.tensor.matmul(turned_w[:, t, :], share[:, t, 1 : P + 1], ident[:], start=True, stop=False, is_transpose=True)
                 nc.tensor.matmul(turned_w[:, t, :], before, ident[:], start=False, stop=True, is_transpose=True)
             weights.append(turned_w)
-        gather_on_vector(0, 3, "shares0")
+        gather_on_vector(0, 2, "got7")
+        gather_on_vector(0, 3, "got6")
         values(1, 1)
         values(1, 0)
         values(0, 0)
@@ -263,47 +263,70 @@ def tile_attend_planecos_stepwise_bysign_pl_kernel(
 
         y_codes = sb("y_codes", [P, Q], U32)
         y_scales = sb("y_scales", [P, Q], U8)
-        for n in range(TILES):
-            w_grouped = sb("w_grouped%d" % n, [P, 2, P, PACK], BF16)
-            for s, op in enumerate((ALU.max, ALU.min)):
-                nc.vector.scalar_tensor_tensor(
-                    out=w_grouped[:, s, :, :], in0=weights[n][:].rearrange("p t q -> p q t"), scalar=0.0,
-                    in1=factor[:].unsqueeze(1).to_broadcast([P, P, PACK]), op0=op, op1=ALU.mult,
-                )
-            w_codes = sb("w_codes%d" % n, [P, 2 * P], U32)
-            w_scales = sb("w_scales%d" % n, [P, 2 * P], U8)
-            nc.vector.quantize_mx(
-                out=w_codes[:].bitcast(FP8X4), scales=w_scales[:], in_=w_grouped[:].rearrange("p s q t -> p (s q t)")
+        w_codes, w_scales = {}, {}
+
+        def signed_weights(n, s):
+            w_grouped = sb("w_grouped%d%d" % (n, s), [P, P, PACK], BF16)
+            nc.vector.scalar_tensor_tensor(
+                out=w_grouped[:], in0=weights[n][:].rearrange("p t q -> p q t"), scalar=0.0,
+                in1=factor[:].unsqueeze(1).to_broadcast([P, P, PACK]), op0=(ALU.max, ALU.min)[s], op1=ALU.mult,
             )
-            result = bank((0, 5)[n], "result", [P, PACK, P])
-            for j in range(PACK):
-                h, jj = divmod(j, 2)
-                for s in range(2):
-                    nc.tensor.matmul_mx(
-                        out=result[:, j, :],
-                        lhsT=v_codes[s, h][:, jj * P : (jj + 1) * P].bitcast(FP8X4),
-                        lhsT_scale=v_scales[s, h][:, jj * P : (jj + 1) * P],
-                        rhs=w_codes[:, s * P : (s + 1) * P].bitcast(FP8X4),
-                        rhs_scale=w_scales[:, s * P : (s + 1) * P],
-                        start=(s == 0),
-                        stop=(s == 1),
-                    )
+            return w_grouped
+
+        def quantize_weights(n, s, w_grouped):
+            w_codes[n, s] = sb("w_codes%d%d" % (n, s), [P, P], U32)
+            w_scales[n, s] = sb("w_scales%d%d" % (n, s), [P, P], U8)
+            nc.vector.quantize_mx(
+                out=w_codes[n, s][:].bitcast(FP8X4), scales=w_scales[n, s][:], in_=w_grouped[:].rearrange("p q t -> p (q t)")
+            )
+
+        def product(dst, n, s, j):
+            h, jj = divmod(j, 2)
+            nc.tensor.matmul_mx(
+                out=dst,
+                lhsT=v_codes[s, h][:, jj * P : (jj + 1) * P].bitcast(FP8X4),
+                lhsT_scale=v_scales[s, h][:, jj * P : (jj + 1) * P],
+                rhs=w_codes[n, s][:].bitcast(FP8X4),
+                rhs_scale=w_scales[n, s][:],
+                start=(s == 0),
+                stop=(s == 1),
+            )
+
+        def hand_out(n, y_out, y_grouped, queue):
             cols = slice(n * P, (n + 1) * P)
-            y_grouped = sb("y_grouped%d" % n, [P, P, PACK], BF16)
-            if n == 0:
-                nc.scalar.copy(out=y_grouped[:], in_=result[:].rearrange("p j q -> p q j"))
-            else:
-                nc.vector.tensor_copy(out=y_grouped[:], in_=result[:].rearrange("p j q -> p q j"))
-            y_out = sb("y_out%d" % n, [P, PACK, P], F32)
-            nc.scalar.copy(out=y_out[:], in_=result[:])
-            nc.sync.dma_start(out=out_0.rearrange("(p j) q -> p j q", j=PACK)[:, :, cols], in_=y_out[:])
             nc.vector.quantize_mx(
                 out=y_codes[:, cols].bitcast(FP8X4), scales=y_scales[:, cols], in_=y_grouped[:].rearrange("p q j -> p (q j)")
             )
-            nc.sync.dma_start(
+            queue.dma_start(
                 out=out_1[0].rearrange("p q r -> p (q r)")[:, 4 * n * P : 4 * (n + 1) * P].bitcast(I32),
                 in_=y_codes[:, cols].bitcast(I32),
             )
+
+        out_rows = out_0.rearrange("(p j) q -> p j q", j=PACK)
+        y_out = [sb("y_out%d" % n, [P, PACK, P], F32) for n in range(TILES)]
+        grouped = [signed_weights(0, s) for s in range(2)]
+        for s in range(2):
+            quantize_weights(0, s, grouped[s])
+        result = bank(0, "result", [P, PACK, P])
+        for j in range(PACK):
+            for s in range(2):
+                product(result[:, j, :], 0, s, j)
+        nc.scalar.copy(out=y_out[0][:], in_=result[:])
+        nc.sync.dma_start(out=out_rows[:, :, 0:P], in_=y_out[0][:])
+
+        results = [bank(b, "result_j", [P, P]) for b in (5, 3, 6, 7)]
+        for s in range(2):
+            quantize_weights(1, s, signed_weights(1, s))
+            for j in range(PACK):
+                product(results[j][:], 1, s, j)
+        y_grouped = [sb("y_grouped%d" % n, [P, P, PACK], BF16, tag=("w_grouped10", None)[n]) for n in range(TILES)]
+        nc.scalar.copy(out=y_grouped[0][:], in_=result[:].rearrange("p j q -> p q j"))
+        hand_out(0, y_out[0], y_grouped[0], nc.sync)
+        for j in range(PACK):
+            nc.vector.tensor_copy(out=y_out[1][:, j, :], in_=results[j][:])
+        nc.sync.dma_start(out=out_rows[:, :, P : 2 * P], in_=y_out[1][:])
+        nc.vector.tensor_copy(out=y_grouped[1][:], in_=y_out[1][:].rearrange("p j q -> p q j"))
+        hand_out(1, y_out[1], y_grouped[1], nc.scalar)
         for g in range(4):
             queue = (nc.sync, nc.scalar)[g % 2]
             queue.dma_start(

@@ -16,13 +16,13 @@ FP8X4 = mybir.dt.float8_e4m3fn_x4
 FP4X4 = mybir.dt.float4_e2m1fn_x4
 ALU = mybir.AluOpType
 ACT = mybir.ActivationFunctionType
-AX = mybir.AxisListType
 
 P = 128
 PACK = 4
 BANK = 512
 TILES = Q // P
 CHUNKS = T // BANK
+QUADRANTS = 4
 
 
 def tile_attend_planecos_stepwise_bysign_pl_kernel(
@@ -48,77 +48,64 @@ def tile_attend_planecos_stepwise_bysign_pl_kernel(
             nc.sync.dma_start(out=q_raw[s, n][:], in_=src[:, :, n * P : (n + 1) * P])
 
         key_words = sb("key_words", [P, 2 * T], U8)
-        lists = [keep.tile([P, I // 16], U16, name="list%d" % s, tag="list%d" % s) for s in range(3)]
+        lists = [keep.tile([P, I // 16], U16, name="list%d" % k, tag="list%d" % k) for k in range(3)]
         nc.sync.dma_start(lists[0][:], offs)
         nc.sync.dma_start(lists[1][:], offs2)
         nc.sync.dma_start(lists[2][:], offs3)
         load_queries(0, 0)
         nc.sync.dma_start(out=key_words[:].bitcast(I32), in_=keys_words[0].bitcast(I32))
-        for g in range(4):
+        for g in range(QUADRANTS):
             nc.sync.dma_start(
                 out=key_scales[32 * g : 32 * g + 4, :].bitcast(I32), in_=keys_scales[0][4 * g : 4 * g + 4, :].bitcast(I32)
             )
         load_queries(1, 0)
         load_queries(0, 1)
         load_queries(1, 1)
-        pools = []
-        for s, width in enumerate((T, X)):
-            pools.append([sb("pool%d_%d" % (s, j), [P, width], F32) for j in range(PACK)])
+        stores = [[sb("pool%d_%d" % (s, j), [P, width], F32) for j in range(PACK)] for s, width in enumerate((T, X))]
         lam_col = sb("lam_col", [P, TILES], F32)
         pull_col = sb("pull_col", [P, TILES], F32)
         factor = sb("factor", [P, PACK], F32)
         for j in range(PACK):
-            nc.sync.dma_start(out=pools[1][j][:], in_=vals2.rearrange("(p j) t -> p j t", j=PACK)[:, j, :])
+            nc.sync.dma_start(out=stores[1][j][:], in_=vals2.rearrange("(p j) t -> p j t", j=PACK)[:, j, :])
         with nc.allow_non_contiguous_dma(reason="one number a query row"):
             nc.sync.dma_start(out=lam_col[:], in_=lam.rearrange("(t p) o -> p (t o)", p=P))
             nc.sync.dma_start(out=pull_col[:], in_=pull.rearrange("(t p) o -> p (t o)", p=P))
         nc.sync.dma_start(out=factor[:], in_=slot_factor.rearrange("o (p t) -> p (o t)", t=PACK))
         for j in range(PACK):
-            nc.sync.dma_start(out=pools[0][j][:], in_=vals.rearrange("(p j) t -> p j t", j=PACK)[:, j, :])
+            nc.sync.dma_start(out=stores[0][j][:], in_=vals.rearrange("(p j) t -> p j t", j=PACK)[:, j, :])
 
         warm = sb("warm", [P, 2], F32)
         nc.vector.memset(warm[:, 0:1], 1.0)
         nc.scalar.activation(out=warm[:, 1:2], in_=warm[:, 0:1], func=ACT.Abs_reciprocal_sqrt)
         ident = sb("ident", [P, P], F32)
         make_identity(nc, ident[:])
-        shares = [sb("shares%d" % n, [P, PACK, P + 1], F32) for n in range(TILES)]
+        exps = [sb("shares%d" % n, [P, PACK, P + 1], F32) for n in range(TILES)]
         for n in range(TILES):
-            nc.gpsimd.memset(shares[n][:, :, 0:1], 0.0)
+            nc.gpsimd.memset(exps[n][:, :, 0:1], 0.0)
         neg_pull = sb("neg_pull", [P, TILES], F32)
         nc.gpsimd.tensor_scalar(out=neg_pull[:], in0=pull_col[:], scalar1=-1.0, scalar2=0.0, op0=ALU.mult, op1=ALU.add)
-
         neg_lam = sb("neg_lam", [P, TILES], F32)
         nc.gpsimd.tensor_scalar(out=neg_lam[:], in0=lam_col[:], scalar1=-1.0, scalar2=0.0, op0=ALU.mult, op1=ALU.add)
-        got = {}
-
-        def gather_on_scalar(j, tag):
-            got[1, j] = sb("got1%d" % j, [P, I], BF16, tag=tag)
-            nc.scalar.activation(out=got[1, j][:], in_=rounded[j][:].indirect(lists[2][:]), func=ACT.Copy)
-
-        def gather_on_vector(s, j, tag):
-            got[s, j] = sb("got%d%d" % (s, j), [P, I], BF16, tag=tag)
-            nc.vector.tensor_copy(out=got[s, j][:], in_=pools[s][j][:].indirect(lists[2 * s][:]))
 
         q_codes, q_scales = {}, {}
         for s, n in ((0, 0), (1, 0), (0, 1), (1, 1)):
-            grouped = sb("q_grouped%d%d" % (s, n), [P, P, PACK], BF16)
-            nc.vector.tensor_copy(out=grouped[:], in_=q_raw[s, n][:].rearrange("p j q -> p q j"))
+            q_grouped = sb("q_grouped%d%d" % (s, n), [P, P, PACK], BF16)
+            nc.vector.tensor_copy(out=q_grouped[:], in_=q_raw[s, n][:].rearrange("p j q -> p q j"))
             q_codes[s, n] = sb("q_codes%d%d" % (s, n), [P, P], U32)
             q_scales[s, n] = sb("q_scales%d%d" % (s, n), [P, P], U8)
             nc.vector.quantize_mx(
-                out=q_codes[s, n][:].bitcast(FP8X4), scales=q_scales[s, n][:], in_=grouped[:].rearrange("p q j -> p (q j)")
+                out=q_codes[s, n][:].bitcast(FP8X4), scales=q_scales[s, n][:], in_=q_grouped[:].rearrange("p q j -> p (q j)")
             )
 
-        rounded = {0: sb("rounded0", [P, X], BF16, tag="q_grouped11")}
-        for c in range(2):
-            nc.gpsimd.tensor_copy(out=rounded[0][:, c * BANK : (c + 1) * BANK], in_=pools[1][0][:, c * BANK : (c + 1) * BANK])
+        rounded = sb("rounded0", [P, X], BF16, tag="q_grouped11")
+        for c in range(X // BANK):
+            nc.gpsimd.tensor_copy(out=rounded[:, c * BANK : (c + 1) * BANK], in_=stores[1][0][:, c * BANK : (c + 1) * BANK])
 
-        points = {}
         picked = [sb("picked%d" % n, [P, 4, I], F32) for n in range(TILES)]
         squares = [sb("squares%d" % n, [P, 4, I], F32) for n in range(TILES)]
         for n in range(TILES):
             for s in range(2):
-                points[s, n] = sb("points%d%d" % (s, n), [P, T], F32)
+                points = sb("points%d%d" % (s, n), [P, T], F32)
                 for c in range(CHUNKS):
                     acc = bank(c, "acc", [P, BANK])
                     nc.tensor.matmul_mx(
@@ -130,22 +117,22 @@ def tile_attend_planecos_stepwise_bysign_pl_kernel(
                         start=True,
                         stop=True,
                     )
-                    dst = points[s, n][:, c * BANK : (c + 1) * BANK]
+                    dst = points[:, c * BANK : (c + 1) * BANK]
                     if (n, s) == (0, 0) and c % 2 == 1:
                         nc.vector.tensor_copy(out=dst, in_=acc[:])
                     else:
                         nc.scalar.copy(out=dst, in_=acc[:])
                 for k in range(2):
-                    nc.vector.tensor_copy(out=picked[n][:, 2 * s + k, :], in_=points[s, n][:].indirect(lists[k][:]))
+                    nc.vector.tensor_copy(out=picked[n][:, 2 * s + k, :], in_=points[:].indirect(lists[k][:]))
+
+        la_bank, lb_bank, dot_bank = (4, 6), (5, 7), 4
+        la_out, lb, dot, root, neg_scores, neg_max, gathered = {}, {}, {}, {}, {}, {}, {}
 
         def turn_sum(dst, first, second):
-            for c in range(PACK):
+            for c in range(I // P):
                 cols = slice(c * P, (c + 1) * P)
                 nc.tensor.matmul(dst[:, c, :], first[:, cols], ident[:], start=True, stop=False, is_transpose=True)
                 nc.tensor.matmul(dst[:, c, :], second[:, cols], ident[:], start=False, stop=True, is_transpose=True)
-
-        base = (4, 6)
-        dots, inv, las, lbs, lengths = {}, {}, {}, {}, {}
 
         def square(n, first, count):
             part = picked[n][:, first : first + count, :]
@@ -154,72 +141,105 @@ def tile_attend_planecos_stepwise_bysign_pl_kernel(
             else:
                 nc.scalar.activation(out=squares[n][:, first : first + count, :], in_=part, func=ACT.Square)
 
-        def sum_first(n):
-            la = bank(base[n], "la", [P, PACK, P])
+        def sum_la(n):
+            la = bank(la_bank[n], "la", [P, PACK, P])
             turn_sum(la, squares[n][:, 0, :], squares[n][:, 2, :])
-            las[n] = sb("la_sb%d" % n, [P, PACK, P], F32, tag=("got2", "got8")[n])
-            nc.scalar.copy(out=las[n][:], in_=la[:])
+            la_out[n] = sb("la_sb%d" % n, [P, PACK, P], F32, tag=("got2", "got8")[n])
+            nc.scalar.copy(out=la_out[n][:], in_=la[:])
 
-        def sum_second(n):
-            lbs[n] = bank(base[n] + 1, "lb", [P, PACK, P])
-            turn_sum(lbs[n], squares[n][:, 1, :], squares[n][:, 3, :])
+        def sum_lb(n):
+            lb[n] = bank(lb_bank[n], "lb", [P, PACK, P])
+            turn_sum(lb[n], squares[n][:, 1, :], squares[n][:, 3, :])
 
         def dot_product(n):
             products = sb("products%d" % n, [P, 2, I], F32)
             for s in range(2):
                 nc.gpsimd.tensor_tensor(out=products[:, s, :], in0=picked[n][:, 2 * s, :], in1=picked[n][:, 2 * s + 1, :], op=ALU.mult)
-            dots[n] = bank(4, "dot", [P, PACK, P])
-            turn_sum(dots[n], products[:, 0, :], products[:, 1, :])
+            dot[n] = bank(dot_bank, "dot", [P, PACK, P])
+            turn_sum(dot[n], products[:, 0, :], products[:, 1, :])
 
         def inverse_root(n):
-            lengths[n] = sb("lengths%d" % n, [P, PACK, P], F32, tag=(None, "got7")[n])
-            nc.vector.tensor_tensor(out=lengths[n][:], in0=lbs[n][:], in1=las[n][:], op=ALU.mult)
-            inv[n] = sb("root%d" % n, [P, PACK, P], F32, tag=("got3", "got4")[n])
-            nc.scalar.activation(out=inv[n][:], in_=lengths[n][:], func=ACT.Abs_reciprocal_sqrt, bias=0.5)
-
-        scores, neg_max = [], []
+            lengths = sb("lengths%d" % n, [P, PACK, P], F32, tag=(None, "got7")[n])
+            nc.vector.tensor_tensor(out=lengths[:], in0=lb[n][:], in1=la_out[n][:], op=ALU.mult)
+            root[n] = sb("root%d" % n, [P, PACK, P], F32, tag=("got3", "got4")[n])
+            nc.scalar.activation(out=root[n][:], in_=lengths[:], func=ACT.Abs_reciprocal_sqrt, bias=0.5)
 
         def row_scores(n):
             turned = sb("turned%d" % n, [P, PACK, P], F32)
-            nc.vector.tensor_tensor(out=turned[:], in0=dots[n][:], in1=inv[n][:], op=ALU.mult)
-            score = bank(n, "score", [P, PACK, P])
-            for c in range(PACK):
-                nc.tensor.transpose(score[:, c, :], turned[:, c, :], ident[:])
-            top = sb("top%d" % n, [P, 1], F32)
-            neg_score = sb("neg_score%d" % n, [P, PACK, P], F32)
+            nc.vector.tensor_tensor(out=turned[:], in0=dot[n][:], in1=root[n][:], op=ALU.mult)
+            cosine = bank(n, "score", [P, PACK, P])
+            for c in range(I // P):
+                nc.tensor.transpose(cosine[:, c, :], turned[:, c, :], ident[:])
+            neg_max[n] = sb("top%d" % n, [P, 1], F32)
+            neg_scores[n] = sb("neg_score%d" % n, [P, PACK, P], F32)
             nc.vector.tensor_scalar(
-                out=neg_score[:], in0=score[:].rearrange("q c p -> q (c p)").rearrange("q (p t) -> q t p", t=PACK),
-                scalar1=neg_lam[:, n : n + 1], scalar2=None, op0=ALU.mult, op1=ALU.min, accum_out=top[:],
+                out=neg_scores[n][:], in0=cosine[:].rearrange("q c p -> q (c p)").rearrange("q (p t) -> q t p", t=PACK),
+                scalar1=neg_lam[:, n : n + 1], scalar2=None, op0=ALU.mult, op1=ALU.min, accum_out=neg_max[n][:],
             )
-            scores.append(neg_score)
-            neg_max.append(top)
 
-        gather_on_vector(1, 2, "points10")
+        def gather_values(s, j, tag):
+            gathered[s, j] = sb("got%d%d" % (s, j), [P, I], BF16, tag=tag)
+            nc.vector.tensor_copy(out=gathered[s, j][:], in_=stores[s][j][:].indirect(lists[2 * s][:]))
+
+        gather_values(1, 2, "points10")
+        rounded_second = sb("rounded1", [P, X], BF16, tag="key_words")
+        nc.scalar.copy(out=rounded_second[:], in_=stores[1][1][:])
+        gathered[1, 1] = sb("got11", [P, I], BF16)
+        nc.scalar.activation(out=gathered[1, 1][:], in_=rounded_second[:].indirect(lists[2][:]), func=ACT.Copy)
         square(0, 0, 2)
         square(0, 2, 2)
-        sum_first(0)
-        sum_second(0)
+        sum_la(0)
+        sum_lb(0)
         square(1, 0, 2)
         square(1, 2, 1)
-        sum_first(1)
+        sum_la(1)
         square(1, 3, 1)
-        sum_second(1)
+        sum_lb(1)
         dot_product(0)
         inverse_root(0)
         inverse_root(1)
         row_scores(0)
         dot_product(1)
         row_scores(1)
-        gather_on_scalar(0, "squares1")
+        gathered[1, 0] = sb("got10", [P, I], BF16, tag="squares1")
+        nc.scalar.activation(out=gathered[1, 0][:], in_=rounded[:].indirect(lists[2][:]), func=ACT.Copy)
+        gather_values(1, 3, "got2")
+        gather_values(0, 0, "got3")
+        gather_values(0, 1, "got8")
+        gather_values(0, 2, "got4")
+
+        weights = []
+        for n in range(TILES):
+            total = sb("total%d" % n, [P, 1], F32, tag=("got7", None)[n])
+            nc.scalar.activation(
+                out=exps[n][:, :, 1 : P + 1], in_=neg_scores[n][:], func=ACT.Exp, scale=-1.0,
+                bias=neg_max[n][:], accum_out=total[:],
+            )
+            norm = sb("norm%d" % n, [P, 1], F32)
+            nc.vector.reciprocal(out=norm[:], in_=total[:])
+            share = sb("share%d" % n, [P, PACK, P + 1], F32)
+            pulled = sb("pulled%d" % n, [P, PACK, P + 1], F32)
+            nc.scalar.activation(out=share[:], in_=exps[n][:], func=ACT.Copy, scale=norm[:])
+            nc.gpsimd.tensor_scalar(
+                out=pulled[:], in0=exps[n][:], scalar1=norm[:], scalar2=neg_pull[:, n : n + 1], op0=ALU.mult, op1=ALU.mult
+            )
+            turned_w = bank((2, dot_bank)[n], "weights", [P, PACK, P])
+            for t in range(PACK):
+                before = pulled[:, t - 1, 1 : P + 1] if t > 0 else pulled[:, PACK - 1, 0:P]
+                nc.tensor.matmul(turned_w[:, t, :], share[:, t, 1 : P + 1], ident[:], start=True, stop=False, is_transpose=True)
+                nc.tensor.matmul(turned_w[:, t, :], before, ident[:], start=False, stop=True, is_transpose=True)
+            weights.append(turned_w)
+        gather_values(0, 3, "got7")
+
         v_codes, v_scales = {}, {}
 
-        def values(s, h):
-            turned_v = bank({(1, 0): 6, (1, 1): 7, (0, 0): 1, (0, 1): 1}[s, h], "turned_v", [P, 2, 2, P])
+        def quantize_values(s, h, b, tag):
+            turned_v = bank(b, "turned_v", [P, 2, 2, P])
             for jj in range(2):
-                words = got[s, 2 * h + jj][:].bitcast(F32)
+                words = gathered[s, 2 * h + jj][:].bitcast(F32)
                 for u in range(2):
                     nc.tensor.transpose(turned_v[:, jj, u, :], words[:, u::2], ident[:])
-            v_grouped = sb("v_grouped%d%d" % (s, h), [P, 2 * P * PACK], BF16, tag={(0, 0): "neg_score1", (0, 1): "share0"}.get((s, h)))
+            v_grouped = sb("v_grouped%d%d" % (s, h), [P, 2 * P * PACK], BF16, tag=tag)
             nc.scalar.copy(
                 out=v_grouped[:].bitcast(F32).rearrange("p (j m u) -> p j m u", j=2, u=2),
                 in_=turned_v[:].rearrange("p j u m -> p j m u"),
@@ -228,38 +248,10 @@ def tile_attend_planecos_stepwise_bysign_pl_kernel(
             v_scales[s, h] = sb("v_scales%d%d" % (s, h), [P, 2 * P], U8)
             nc.vector.quantize_mx(out=v_codes[s, h][:].bitcast(FP8X4), scales=v_scales[s, h][:], in_=v_grouped[:])
 
-        gather_on_vector(1, 3, "got2")
-        gather_on_vector(1, 1, "got3")
-        gather_on_vector(0, 0, "got8")
-        gather_on_vector(0, 1, "got4")
-        norms, weights = [], []
-        for n in range(TILES):
-            total = sb("total%d" % n, [P, 1], F32, tag=("got7", "got6")[n])
-            nc.scalar.activation(
-                out=shares[n][:, :, 1 : P + 1], in_=scores[n][:], func=ACT.Exp, scale=-1.0,
-                bias=neg_max[n][:], accum_out=total[:],
-            )
-            norm = sb("norm%d" % n, [P, 1], F32)
-            nc.vector.reciprocal(out=norm[:], in_=total[:])
-            norms.append(norm)
-            share = sb("share%d" % n, [P, PACK, P + 1], F32)
-            pulled = sb("pulled%d" % n, [P, PACK, P + 1], F32)
-            nc.scalar.activation(out=share[:], in_=shares[n][:], func=ACT.Copy, scale=norms[n][:])
-            nc.gpsimd.tensor_scalar(
-                out=pulled[:], in0=shares[n][:], scalar1=norms[n][:], scalar2=neg_pull[:, n : n + 1], op0=ALU.mult, op1=ALU.mult
-            )
-            turned_w = bank((2, 4)[n], "weights", [P, PACK, P])
-            for t in range(PACK):
-                before = pulled[:, t - 1, 1 : P + 1] if t > 0 else pulled[:, PACK - 1, 0:P]
-                nc.tensor.matmul(turned_w[:, t, :], share[:, t, 1 : P + 1], ident[:], start=True, stop=False, is_transpose=True)
-                nc.tensor.matmul(turned_w[:, t, :], before, ident[:], start=False, stop=True, is_transpose=True)
-            weights.append(turned_w)
-        gather_on_vector(0, 2, "got7")
-        gather_on_vector(0, 3, "got6")
-        values(1, 1)
-        values(1, 0)
-        values(0, 0)
-        values(0, 1)
+        quantize_values(1, 1, lb_bank[1], None)
+        quantize_values(1, 0, la_bank[1], None)
+        quantize_values(0, 0, 1, "neg_score1")
+        quantize_values(0, 1, 1, "share0")
 
         y_codes = sb("y_codes", [P, Q], U32)
         y_scales = sb("y_scales", [P, Q], U8)
@@ -292,18 +284,19 @@ def tile_attend_planecos_stepwise_bysign_pl_kernel(
                 stop=(s == 1),
             )
 
-        def hand_out(n, y_out, y_grouped, queue):
+        def store_codes(n, y_grouped, queue):
             cols = slice(n * P, (n + 1) * P)
             nc.vector.quantize_mx(
                 out=y_codes[:, cols].bitcast(FP8X4), scales=y_scales[:, cols], in_=y_grouped[:].rearrange("p q j -> p (q j)")
             )
             queue.dma_start(
-                out=out_1[0].rearrange("p q r -> p (q r)")[:, 4 * n * P : 4 * (n + 1) * P].bitcast(I32),
+                out=out_1[0].rearrange("p q r -> p (q r)")[:, PACK * n * P : PACK * (n + 1) * P].bitcast(I32),
                 in_=y_codes[:, cols].bitcast(I32),
             )
 
         out_rows = out_0.rearrange("(p j) q -> p j q", j=PACK)
         y_out = [sb("y_out%d" % n, [P, PACK, P], F32) for n in range(TILES)]
+
         grouped = [signed_weights(0, s) for s in range(2)]
         for s in range(2):
             quantize_weights(0, s, grouped[s])
@@ -321,13 +314,13 @@ def tile_attend_planecos_stepwise_bysign_pl_kernel(
                 product(results[j][:], 1, s, j)
         y_grouped = [sb("y_grouped%d" % n, [P, P, PACK], BF16, tag=("w_grouped10", None)[n]) for n in range(TILES)]
         nc.scalar.copy(out=y_grouped[0][:], in_=result[:].rearrange("p j q -> p q j"))
-        hand_out(0, y_out[0], y_grouped[0], nc.sync)
+        store_codes(0, y_grouped[0], nc.sync)
         for j in range(PACK):
             nc.vector.tensor_copy(out=y_out[1][:, j, :], in_=results[j][:])
         nc.sync.dma_start(out=out_rows[:, :, P : 2 * P], in_=y_out[1][:])
         nc.vector.tensor_copy(out=y_grouped[1][:], in_=y_out[1][:].rearrange("p j q -> p q j"))
-        hand_out(1, y_out[1], y_grouped[1], nc.scalar)
-        for g in range(4):
+        store_codes(1, y_grouped[1], nc.scalar)
+        for g in range(QUADRANTS):
             queue = (nc.sync, nc.scalar)[g % 2]
             queue.dma_start(
                 out=out_2[0][4 * g : 4 * g + 4, :].bitcast(I32), in_=y_scales[32 * g : 32 * g + 4, :].bitcast(I32)

from contextlib import ExitStack

import concourse.mybir as mybir
from concourse.masks import make_identity

D, T, I, Q, E, X = 512, 2048, 512, 256, 512, 1024
FLOPS = 2 * (2 * Q * T * D + 2 * E * Q * I)

F32 = mybir.dt.float32
BF16 = mybir.dt.bfloat16
I32 = mybir.dt.int32
U32 = mybir.dt.uint32
U16 = mybir.dt.uint16
U8 = mybir.dt.uint8
FP8X4 = mybir.dt.float8_e4m3fn_x4
FP4X4 = mybir.dt.float4_e2m1fn_x4
ALU = mybir.AluOpType
ACT = mybir.ActivationFunctionType

P = 128
PACK = 4
BANK = 512
TILES = Q // P
CHUNKS = T // BANK
QUADRANTS = 4


def tile_attend_planecos_stepwise_bysign_pl_kernel(
    tc, query, query2, keys_words, keys_scales, lam, pull, slot_factor, vals, vals2, offs, offs2, offs3, out_0, out_1, out_2
):
    nc = tc.nc
    with ExitStack() as ctx:
        keep = ctx.enter_context(tc.tile_pool(name="keep", bufs=1))
        psum = ctx.enter_context(tc.psum_pool(name="psum", bufs=1))

        def sb(name, shape, dtype, tag=None):
            return keep.tile(shape, dtype, name=name, tag=tag or name, align_bytes=64)

        def bank(b, name, shape):
            return psum.tile(shape, F32, name=name, tag="bank%d" % b)

        key_scales = sb("key_scales", [P, T], U8)
        nc.gpsimd.memset(key_scales[:].bitcast(U32), 0)
        q_raw = {(s, n): sb("q_raw%d%d" % (s, n), [P, PACK, P], F32) for s in range(2) for n in range(TILES)}

        def load_queries(s, n):
            src = (query, query2)[s].rearrange("(p j) q -> p j q", j=PACK)
            nc.sync.dma_start(out=q_raw[s, n][:], in_=src[:, :, n * P : (n + 1) * P])

        key_words = sb("key_words", [P, 2 * T], U8)
        lists = [keep.tile([P, I // 16], U16, name="list%d" % k, tag="list%d" % k) for k in range(3)]
        nc.sync.dma_start(lists[0][:], offs)
        nc.sync.dma_start(lists[1][:], offs2)
        nc.sync.dma_start(lists[2][:], offs3)
        load_queries(0, 0)
        nc.sync.dma_start(out=key_words[:].bitcast(I32), in_=keys_words[0].bitcast(I32))
        for g in range(QUADRANTS):
            nc.sync.dma_start(
                out=key_scales[32 * g : 32 * g + 4, :].bitcast(I32), in_=keys_scales[0][4 * g : 4 * g + 4, :].bitcast(I32)
            )
        load_queries(1, 0)
        load_queries(0, 1)
        load_queries(1, 1)
        stores = [[sb("pool%d_%d" % (s, j), [P, width], F32) for j in range(PACK)] for s, width in enumerate((T, X))]
        lam_col = sb("lam_col", [P, TILES], F32)
        pull_col = sb("pull_col", [P, TILES], F32)
        factor = sb("factor", [P, PACK], F32)
        for j in range(PACK):
            nc.sync.dma_start(out=stores[1][j][:], in_=vals2.rearrange("(p j) t -> p j t", j=PACK)[:, j, :])
        with nc.allow_non_contiguous_dma(reason="one number a query row"):
            nc.sync.dma_start(out=lam_col[:], in_=lam.rearrange("(t p) o -> p (t o)", p=P))
            nc.sync.dma_start(out=pull_col[:], in_=pull.rearrange("(t p) o -> p (t o)", p=P))
        nc.sync.dma_start(out=factor[:], in_=slot_factor.rearrange("o (p t) -> p (o t)", t=PACK))
        for j in range(PACK):
            nc.sync.dma_start(out=stores[0][j][:], in_=vals.rearrange("(p j) t -> p j t", j=PACK)[:, j, :])

        warm = sb("warm", [P, 2], F32)
        nc.vector.memset(warm[:, 0:1], 1.0)
        nc.scalar.activation(out=warm[:, 1:2], in_=warm[:, 0:1], func=ACT.Abs_reciprocal_sqrt)
        ident = sb("ident", [P, P], F32)
        make_identity(nc, ident[:])
        exps = [sb("shares%d" % n, [P, PACK, P + 1], F32) for n in range(TILES)]
        for n in range(TILES):
            nc.gpsimd.memset(exps[n][:, :, 0:1], 0.0)
        neg_pull = sb("neg_pull", [P, TILES], F32)
        nc.gpsimd.tensor_scalar(out=neg_pull[:], in0=pull_col[:], scalar1=-1.0, scalar2=0.0, op0=ALU.mult, op1=ALU.add)
        neg_lam = sb("neg_lam", [P, TILES], F32)
        nc.gpsimd.tensor_scalar(out=neg_lam[:], in0=lam_col[:], scalar1=-1.0, scalar2=0.0, op0=ALU.mult, op1=ALU.add)

        q_codes, q_scales = {}, {}
        for s, n in ((0, 0), (1, 0), (0, 1), (1, 1)):
            q_grouped = sb("q_grouped%d%d" % (s, n), [P, P, PACK], BF16)
            nc.vector.tensor_copy(out=q_grouped[:], in_=q_raw[s, n][:].rearrange("p j q -> p q j"))
            q_codes[s, n] = sb("q_codes%d%d" % (s, n), [P, P], U32)
            q_scales[s, n] = sb("q_scales%d%d" % (s, n), [P, P], U8)
            nc.vector.quantize_mx(
                out=q_codes[s, n][:].bitcast(FP8X4), scales=q_scales[s, n][:], in_=q_grouped[:].rearrange("p q j -> p (q j)")
            )

        rounded = sb("rounded0", [P, X], BF16, tag="q_grouped11")
        for c in range(X // BANK):
            nc.gpsimd.tensor_copy(out=rounded[:, c * BANK : (c + 1) * BANK], in_=stores[1][0][:, c * BANK : (c + 1) * BANK])

        picked = [sb("picked%d" % n, [P, 4, I], F32) for n in range(TILES)]
        squares = [sb("squares%d" % n, [P, 4, I], F32) for n in range(TILES)]
        for n in range(TILES):
            for s in range(2):
                points = sb("points%d%d" % (s, n), [P, T], F32)
                for c in range(CHUNKS):
                    acc = bank(c, "acc", [P, BANK])
                    nc.tensor.matmul_mx(
                        out=acc[:],
                        lhsT=q_codes[s, n][:].bitcast(FP8X4),
                        lhsT_scale=q_scales[s, n][:],
                        rhs=key_words[:, 2 * c * BANK : 2 * (c + 1) * BANK].bitcast(FP4X4),
                        rhs_scale=key_scales[:, c * BANK : (c + 1) * BANK],
                        start=True,
                        stop=True,
                    )
                    dst = points[:, c * BANK : (c + 1) * BANK]
                    if (n, s) == (0, 0) and c % 2 == 1:
                        nc.vector.tensor_copy(out=dst, in_=acc[:])
                    else:
                        nc.scalar.copy(out=dst, in_=acc[:])
                for k in range(2):
                    nc.vector.tensor_copy(out=picked[n][:, 2 * s + k, :], in_=points[:].indirect(lists[k][:]))

        la_bank, lb_bank, dot_bank = (4, 6), (5, 7), 4
        la_out, lb, dot, root, neg_scores, neg_max, gathered = {}, {}, {}, {}, {}, {}, {}

        def turn_sum(dst, first, second):
            for c in range(I // P):
                cols = slice(c * P, (c + 1) * P)
                nc.tensor.matmul(dst[:, c, :], first[:, cols], ident[:], start=True, stop=False, is_transpose=True)
                nc.tensor.matmul(dst[:, c, :], second[:, cols], ident[:], start=False, stop=True, is_transpose=True)

        def square(n, first, count):
            part = picked[n][:, first : first + count, :]
            if n == 0:
                nc.gpsimd.tensor_tensor(out=squares[n][:, first : first + count, :], in0=part, in1=part, op=ALU.mult)
            else:
                nc.scalar.activation(out=squares[n][:, first : first + count, :], in_=part, func=ACT.Square)

        def sum_la(n):
            la = bank(la_bank[n], "la", [P, PACK, P])
            turn_sum(la, squares[n][:, 0, :], squares[n][:, 2, :])
            la_out[n] = sb("la_sb%d" % n, [P, PACK, P], F32, tag=("got2", "got8")[n])
            nc.scalar.copy(out=la_out[n][:], in_=la[:])

        def sum_lb(n):
            lb[n] = bank(lb_bank[n], "lb", [P, PACK, P])
            turn_sum(lb[n], squares[n][:, 1, :], squares[n][:, 3, :])

        def dot_product(n):
            products = sb("products%d" % n, [P, 2, I], F32)
            for s in range(2):
                nc.gpsimd.tensor_tensor(out=products[:, s, :], in0=picked[n][:, 2 * s, :], in1=picked[n][:, 2 * s + 1, :], op=ALU.mult)
            dot[n] = bank(dot_bank, "dot", [P, PACK, P])
            turn_sum(dot[n], products[:, 0, :], products[:, 1, :])

        def inverse_root(n):
            lengths = sb("lengths%d" % n, [P, PACK, P], F32, tag=(None, "got7")[n])
            nc.vector.tensor_tensor(out=lengths[:], in0=lb[n][:], in1=la_out[n][:], op=ALU.mult)
            root[n] = sb("root%d" % n, [P, PACK, P], F32, tag=("got3", "got4")[n])
            nc.scalar.activation(out=root[n][:], in_=lengths[:], func=ACT.Abs_reciprocal_sqrt, bias=0.5)

        def row_scores(n):
            turned = sb("turned%d" % n, [P, PACK, P], F32)
            nc.vector.tensor_tensor(out=turned[:], in0=dot[n][:], in1=root[n][:], op=ALU.mult)
            cosine = bank(n, "score", [P, PACK, P])
            for c in range(I // P):
                nc.tensor.transpose(cosine[:, c, :], turned[:, c, :], ident[:])
            neg_max[n] = sb("top%d" % n, [P, 1], F32)
            neg_scores[n] = sb("neg_score%d" % n, [P, PACK, P], F32)
            nc.vector.tensor_scalar(
                out=neg_scores[n][:], in0=cosine[:].rearrange("q c p -> q (c p)").rearrange("q (p t) -> q t p", t=PACK),
                scalar1=neg_lam[:, n : n + 1], scalar2=None, op0=ALU.mult, op1=ALU.min, accum_out=neg_max[n][:],
            )

        def gather_values(s, j, tag):
            gathered[s, j] = sb("got%d%d" % (s, j), [P, I], BF16, tag=tag)
            nc.vector.tensor_copy(out=gathered[s, j][:], in_=stores[s][j][:].indirect(lists[2 * s][:]))

        gather_values(1, 2, "points10")
        rounded_second = sb("rounded1", [P, X], BF16, tag="key_words")
        nc.scalar.copy(out=rounded_second[:], in_=stores[1][1][:])
        gathered[1, 1] = sb("got11", [P, I], BF16)
        nc.scalar.activation(out=gathered[1, 1][:], in_=rounded_second[:].indirect(lists[2][:]), func=ACT.Copy)
        square(0, 0, 2)
        square(0, 2, 2)
        sum_la(0)
        sum_lb(0)
        square(1, 0, 2)
        square(1, 2, 1)
        sum_la(1)
        square(1, 3, 1)
        sum_lb(1)
        dot_product(0)
        inverse_root(0)
        inverse_root(1)
        row_scores(0)
        dot_product(1)
        row_scores(1)
        gathered[1, 0] = sb("got10", [P, I], BF16, tag="squares1")
        nc.scalar.activation(out=gathered[1, 0][:], in_=rounded[:].indirect(lists[2][:]), func=ACT.Copy)
        gather_values(1, 3, "got2")
        gather_values(0, 0, "got3")
        gather_values(0, 1, "got8")
        gather_values(0, 2, "got4")

        weights = []
        for n in range(TILES):
            total = sb("total%d" % n, [P, 1], F32, tag=("got7", None)[n])
            nc.scalar.activation(
                out=exps[n][:, :, 1 : P + 1], in_=neg_scores[n][:], func=ACT.Exp, scale=-1.0,
                bias=neg_max[n][:], accum_out=total[:],
            )
            norm = sb("norm%d" % n, [P, 1], F32)
            nc.vector.reciprocal(out=norm[:], in_=total[:])
            share = sb("share%d" % n, [P, PACK, P + 1], F32)
            pulled = sb("pulled%d" % n, [P, PACK, P + 1], F32)
            nc.scalar.activation(out=share[:], in_=exps[n][:], func=ACT.Copy, scale=norm[:])
            nc.gpsimd.tensor_scalar(
                out=pulled[:], in0=exps[n][:], scalar1=norm[:], scalar2=neg_pull[:, n : n + 1], op0=ALU.mult, op1=ALU.mult
            )
            turned_w = bank((2, dot_bank)[n], "weights", [P, PACK, P])
            for t in range(PACK):
                before = pulled[:, t - 1, 1 : P + 1] if t > 0 else pulled[:, PACK - 1, 0:P]
                nc.tensor.matmul(turned_w[:, t, :], share[:, t, 1 : P + 1], ident[:], start=True, stop=False, is_transpose=True)
                nc.tensor.matmul(turned_w[:, t, :], before, ident[:], start=False, stop=True, is_transpose=True)
            weights.append(turned_w)
        gather_values(0, 3, "got7")

        v_codes, v_scales = {}, {}

        def quantize_values(s, h, b, tag):
            turned_v = bank(b, "turned_v", [P, 2, 2, P])
            for jj in range(2):
                words = gathered[s, 2 * h + jj][:].bitcast(F32)
                for u in range(2):
                    nc.tensor.transpose(turned_v[:, jj, u, :], words[:, u::2], ident[:])
            v_grouped = sb("v_grouped%d%d" % (s, h), [P, 2 * P * PACK], BF16, tag=tag)
            nc.scalar.copy(
                out=v_grouped[:].bitcast(F32).rearrange("p (j m u) -> p j m u", j=2, u=2),
                in_=turned_v[:].rearrange("p j u m -> p j m u"),
            )
            v_codes[s, h] = sb("v_codes%d%d" % (s, h), [P, 2 * P], U32)
            v_scales[s, h] = sb("v_scales%d%d" % (s, h), [P, 2 * P], U8)
            nc.vector.quantize_mx(out=v_codes[s, h][:].bitcast(FP8X4), scales=v_scales[s, h][:], in_=v_grouped[:])

        quantize_values(1, 1, lb_bank[1], None)
        quantize_values(1, 0, la_bank[1], None)
        quantize_values(0, 0, 1, "neg_score1")
        quantize_values(0, 1, 1, "share0")

        y_codes = sb("y_codes", [P, Q], U32)
        y_scales = sb("y_scales", [P, Q], U8)
        w_codes, w_scales = {}, {}

        def signed_weights(n, s):
            w_grouped = sb("w_grouped%d%d" % (n, s), [P, P, PACK], BF16)
            nc.vector.scalar_tensor_tensor(
                out=w_grouped[:], in0=weights[n][:].rearrange("p t q -> p q t"), scalar=0.0,
                in1=factor[:].unsqueeze(1).to_broadcast([P, P, PACK]), op0=(ALU.max, ALU.min)[s], op1=ALU.mult,
            )
            return w_grouped

        def quantize_weights(n, s, w_grouped):
            w_codes[n, s] = sb("w_codes%d%d" % (n, s), [P, P], U32)
            w_scales[n, s] = sb("w_scales%d%d" % (n, s), [P, P], U8)
            nc.vector.quantize_mx(
                out=w_codes[n, s][:].bitcast(FP8X4), scales=w_scales[n, s][:], in_=w_grouped[:].rearrange("p q t -> p (q t)")
            )

        def product(dst, n, s, j):
            h, jj = divmod(j, 2)
            nc.tensor.matmul_mx(
                out=dst,
                lhsT=v_codes[s, h][:, jj * P : (jj + 1) * P].bitcast(FP8X4),
                lhsT_scale=v_scales[s, h][:, jj * P : (jj + 1) * P],
                rhs=w_codes[n, s][:].bitcast(FP8X4),
                rhs_scale=w_scales[n, s][:],
                start=(s == 0),
                stop=(s == 1),
            )

        def store_codes(n, y_grouped, queue):
            cols = slice(n * P, (n + 1) * P)
            nc.vector.quantize_mx(
                out=y_codes[:, cols].bitcast(FP8X4), scales=y_scales[:, cols], in_=y_grouped[:].rearrange("p q j -> p (q j)")
            )
            queue.dma_start(
                out=out_1[0].rearrange("p q r -> p (q r)")[:, PACK * n * P : PACK * (n + 1) * P].bitcast(I32),
                in_=y_codes[:, cols].bitcast(I32),
            )

        out_rows = out_0.rearrange("(p j) q -> p j q", j=PACK)
        y_out = [sb("y_out%d" % n, [P, PACK, P], F32) for n in range(TILES)]

        grouped = [signed_weights(0, s) for s in range(2)]
        for s in range(2):
            quantize_weights(0, s, grouped[s])
        result = bank(0, "result", [P, PACK, P])
        for j in range(PACK):
            for s in range(2):
                product(result[:, j, :], 0, s, j)
        nc.scalar.copy(out=y_out[0][:], in_=result[:])
        nc.sync.dma_start(out=out_rows[:, :, 0:P], in_=y_out[0][:])

        results = [bank(b, "result_j", [P, P]) for b in (5, 3, 6, 7)]
        for s in range(2):
            quantize_weights(1, s, signed_weights(1, s))
            for j in range(PACK):
                product(results[j][:], 1, s, j)
        y_grouped = [sb("y_grouped%d" % n, [P, P, PACK], BF16, tag=("w_grouped10", None)[n]) for n in range(TILES)]
        nc.scalar.copy(out=y_grouped[0][:], in_=result[:].rearrange("p j q -> p q j"))
        store_codes(0, y_grouped[0], nc.sync)
        for j in range(PACK):
            nc.vector.tensor_copy(out=y_out[1][:, j, :], in_=results[j][:])
        nc.sync.dma_start(out=out_rows[:, :, P : 2 * P], in_=y_out[1][:])
        nc.vector.tensor_copy(out=y_grouped[1][:], in_=y_out[1][:].rearrange("p j q -> p q j"))
        store_codes(1, y_grouped[1], nc.scalar)
        for g in range(QUADRANTS):
            queue = (nc.sync, nc.scalar)[g % 2]
            queue.dma_start(
                out=out_2[0][4 * g : 4 * g + 4, :].bitcast(I32), in_=y_scales[32 * g : 32 * g + 4, :].bitcast(I32)
            )
